import numpy as np
import ml_dtypes


def mxq(x, axis, fmt="e4m3"):
    dtype, down = {"e4m3": (ml_dtypes.float8_e4m3fn, 7), "e5m2": (ml_dtypes.float8_e5m2, 14)}[fmt]
    v = np.moveaxis(np.asarray(x, np.float32).astype(ml_dtypes.bfloat16).astype(np.float64), axis, -1)
    blocks = v.reshape(v.shape[:-1] + (-1, 32))
    amax = np.abs(blocks).max(-1, keepdims=True)
    byte = np.maximum(np.where(amax > 0, np.frexp(amax)[1] - 1 + 127, 0) - down, 1)
    scale = np.exp2(byte - 127.0)
    codes = (blocks / scale).astype(np.float32).astype(dtype).astype(np.float64)
    return np.moveaxis((codes * scale).reshape(v.shape), -1, axis)


WIDE = False


def mx_kscale(k):
    if not WIDE:
        return np.ones(k)
    levels = np.array([10, -10, 5, -5, 0])
    if k % 512:
        return np.exp2(np.random.permutation(np.resize(levels, k // 32))).repeat(32)
    a = np.empty((k // 512, 16))
    for p in range(k // 512):
        a[p, :8] = np.random.permutation(np.resize(levels, 8))
        for g in range(8):
            far = levels[np.abs(levels - a[p, g]) >= 10]
            a[p, g + 8] = far[np.random.randint(len(far))]
    return np.exp2(a.ravel()).repeat(32)


def f64(x):
    return np.asarray(x).astype(np.float64)


def striped(idx):
    return np.tile(np.asarray(idx).reshape(-1, 16).T, (8, 1)).astype(np.uint16)


def unstriped(offs):
    return offs[:16].T.reshape(-1).astype(np.int64)


E2M1 = np.array([0.0, 0.5, 1.0, 1.5, 2.0, 3.0, 4.0, 6.0, -0.0, -0.5, -1.0, -1.5, -2.0, -3.0, -4.0, -6.0])


def pack_weight(w, fmt):
    k, n = w.shape
    w = f64(np.asarray(w, np.float32).astype(ml_dtypes.bfloat16)).reshape(k // 32, 32, n)
    amax = np.abs(w).max(1)
    if fmt == "e4m3":
        byte = np.frexp(amax)[1] - 1 + 127 - 7
    else:
        mant, ex = np.frexp(amax / 6.0)
        byte = np.where(mant > 0.5, ex, ex - 1) + 127
    byte = np.clip(np.where(amax > 0, byte, 1), 1, 254)
    scaled = (w * np.exp2(127.0 - byte)[:, None, :]).reshape(k, n).astype(np.float32)
    by_word = np.ascontiguousarray(scaled.reshape(k // 512, 128, 4, n).transpose(0, 1, 3, 2))
    if fmt == "e4m3":
        words = by_word.astype(ml_dtypes.float8_e4m3fn).view(np.uint8)
    else:
        c = by_word.astype(ml_dtypes.float4_e2m1fn).view(np.uint8) & 0xF
        words = (c[..., 0::2] | (c[..., 1::2] << 4)).reshape(k // 512, 128, 2 * n)
    return np.ascontiguousarray(words), np.ascontiguousarray(byte.astype(np.uint8).reshape(k // 512, 16, n))


def unpack_weight(words, scales, fmt):
    g, _, n = scales.shape
    words = np.ascontiguousarray(words).reshape(g, 128, n, -1)
    if fmt == "e4m3":
        vals = words.view(ml_dtypes.float8_e4m3fn).astype(np.float64)
    else:
        nib = np.empty((g, 128, n, 4), np.uint8)
        nib[..., 0::2] = words & 0xF
        nib[..., 1::2] = words >> 4
        vals = E2M1[nib]
    vals = vals * np.repeat(np.exp2(scales.astype(np.float64) - 127.0), 8, axis=1)[..., None]
    return vals.transpose(0, 1, 3, 2).reshape(g * 512, n)


def sigmoid(v):
    return 1.0 / (1.0 + np.exp(-v))


def bf(x):
    return np.asarray(x, np.float32).astype(ml_dtypes.bfloat16)


def planes(Y):
    r, m = Y.shape
    b = f64(bf(Y)).reshape(r // 32, 32, m)
    amax = np.abs(b).max(1)
    byte = np.clip(np.where(amax > 0, np.frexp(amax)[1] - 1 + 127 - 7, 1), 1, 254)
    codes = (b * np.exp2(127.0 - byte)[:, None, :]).reshape(r, m).astype(np.float32).astype(ml_dtypes.float8_e4m3fn).view(np.uint8)
    words = codes.reshape(r // 512, 128, 4, m).transpose(0, 1, 3, 2)
    return np.ascontiguousarray(words), np.ascontiguousarray(byte.astype(np.uint8).reshape(r // 512, 16, m))


D, E, T, I, Q, G = 512, 512, 2048, 512, 256, 64


def setup_inputs():
    n = np.random.standard_normal
    idx = np.random.permutation(T)[:I]
    fd = mx_kscale(D)
    fi = mx_kscale(I)
    ti = np.ones(T)
    ti[idx] = fi
    keysp = pack_weight(n((D, T)) / fd[:, None], "e2m1")
    return {
        "query": (n((D, Q)) * 0.6 / np.sqrt(D) * fd[:, None]).astype(np.float32),
        "dquery": (n((D, Q)) * 1.0 / np.sqrt(D) * fd[:, None]).astype(np.float32),
        "keys_words": keysp[0],
        "keys_scales": keysp[1],
        "os": (np.random.uniform(1.0, 4.0, (1, I)) * fi).astype(np.float32),
        "vals": (n((E, T)) / ti).astype(np.float32),
        "offs": striped(idx),
    }


def reference(query, dquery, keys_words, keys_scales, os, vals, offs):
    idx = unstriped(offs)
    keysu = unpack_weight(keys_words, keys_scales, "e2m1")
    queryq = mxq(f64(query), 0, "e4m3")
    keysidxg = keysu[:, idx]
    a = queryq.T @ keysidxg
    dqueryq = mxq(f64(dquery), 0, "e4m3")
    ta = dqueryq.T @ keysidxg
    s = a.reshape(Q, G, I // G).mean(axis=2)
    p = np.exp(s - np.max(s, axis=1, keepdims=True))
    r = p / np.sum(p, axis=1, keepdims=True)
    rr = np.repeat(r, I // G, axis=1)
    ts = ta.reshape(Q, G, I // G).mean(axis=2)
    tp = ts * p
    tr = (tp - np.sum(tp, axis=1, keepdims=True) * p / np.sum(p, axis=1, keepdims=True)) / np.sum(p, axis=1, keepdims=True)
    trr = np.repeat(tr, I // G, axis=1)
    tw = trr * sigmoid(a) + ta * sigmoid(a) * (1.0 - sigmoid(a)) * rr
    wo1 = tw * f64(os)
    wt1 = wo1.T
    vt1 = f64(vals)[:, idx].T
    vt1q = mxq(vt1, 0, "e4m3")
    wt1q = mxq(wt1, 0, "e4m3")
    o = vt1q.T @ wt1q
    words, scales = planes(o)
    return o, words, scales

@@ -1,0 +1,259 @@
+from contextlib import ExitStack
+
+import concourse.mybir as mybir
+from concourse.masks import make_identity
+
+D, E, T, I, Q, G = 512, 512, 2048, 512, 256, 64
+FLOPS = 2 * (2 * Q * D * I + E * I * Q)
+
+F32 = mybir.dt.float32
+BF16 = mybir.dt.bfloat16
+I32 = mybir.dt.int32
+U32 = mybir.dt.uint32
+U16 = mybir.dt.uint16
+U8 = mybir.dt.uint8
+FP8X4 = mybir.dt.float8_e4m3fn_x4
+FP4X4 = mybir.dt.float4_e2m1fn_x4
+ALU = mybir.AluOpType
+ACT = mybir.ActivationFunctionType
+AX = mybir.AxisListType
+
+P = 128
+PACK = 4
+SPAN = I // G
+HALVES = Q // P
+
+
+def tile_attend_ttspanread_pl_kernel(tc, query, dquery, keys_words, keys_scales, slot_factor, vals, offs, out_0, out_1, out_2):
+    nc = tc.nc
+    with ExitStack() as ctx:
+        held = ctx.enter_context(tc.tile_pool(name="held", bufs=1))
+        psum = ctx.enter_context(tc.psum_pool(name="psum", bufs=1))
+
+        def bank(b, shape, name):
+            return psum.tile(shape, F32, name=name, tag="bank%d" % b)
+
+        offsets = held.tile([P, I // 16], U16, name="offsets")
+        nc.sync.dma_start(offsets[:], offs)
+        key_words = held.tile([P, T], U16, name="key_words")
+        nc.sync.dma_start(key_words[:].bitcast(I32), keys_words[0].bitcast(I32))
+        key_bytes = held.tile([P, T], U8, name="key_bytes", tag="bytes_then_codes0", align_bytes=64)
+        nc.vector.memset(key_bytes[:, : T // 2].bitcast(I32), 0)
+        nc.gpsimd.memset(key_bytes[:, T // 2 :].bitcast(I32), 0)
+        q_raw = [held.tile([P, PACK, Q], F32, name="q_raw%d" % n) for n in range(2)]
+        nc.sync.dma_start(q_raw[0][:], query.rearrange("(p j) q -> p j q", j=PACK))
+        for quad in range(4):
+            nc.sync.dma_start(
+                key_bytes[32 * quad : 32 * quad + 4, :].bitcast(I32),
+                keys_scales[0, 4 * quad : 4 * quad + 4, :].bitcast(I32),
+            )
+        nc.sync.dma_start(q_raw[1][:], dquery.rearrange("(p j) q -> p j q", j=PACK))
+        vals_dealt = vals.rearrange("(p t) n -> t p n", t=PACK)
+        v_raw = [held.tile([P, T], F32, name="v_raw%d" % t, tag="plane%d" % t, align_bytes=64) for t in range(PACK)]
+        nc.sync.dma_start(v_raw[0][:], vals_dealt[0])
+        os_col = held.tile([P, PACK], F32, name="os_col")
+        nc.sync.dma_start(os_col[:], slot_factor.rearrange("o (p t) -> (o p) t", t=PACK))
+        for t in range(1, PACK):
+            nc.sync.dma_start(v_raw[t][:], vals_dealt[t])
+
+        ident = held.tile([P, P], F32, name="ident")
+        make_identity(nc, ident[:])
+
+        warm_in = held.tile([P, 1], F32, name="warm_in")
+        nc.vector.memset(warm_in[:], 0.0)
+        warm_out = held.tile([P, 1], F32, name="warm_out")
+        nc.scalar.activation(warm_out[:], warm_in[:], ACT.Sigmoid)
+
+        kg_words = held.tile([P, I], U16, name="kg_words", align_bytes=64)
+        nc.vector.tensor_copy(kg_words[:], key_words[:].indirect(offsets[:]))
+        kg_bytes = held.tile([P, I], U8, name="kg_bytes", align_bytes=64)
+        nc.vector.tensor_copy(kg_bytes[:], key_bytes[:].indirect(offsets[:]))
+
+        q_codes, q_scales = [], []
+        for n in range(2):
+            grouped = held.tile([P, Q, PACK], BF16, name="q_grouped%d" % n, align_bytes=64)
+            nc.scalar.copy(
+                grouped[:].rearrange("p (c i) j -> p c j i", i=4),
+                q_raw[n][:].rearrange("p j (c i) -> p c j i", i=4),
+            )
+            codes = held.tile([P, Q], U32, name="q_codes%d" % n, tag="bytes_then_codes%d" % n, align_bytes=64)
+            scales = held.tile([P, Q], U8, name="q_scales%d" % n, align_bytes=64)
+            nc.vector.quantize_mx(codes[:].bitcast(FP8X4), scales[:], grouped[:].rearrange("p q j -> p (q j)"))
+            q_codes.append(codes)
+            q_scales.append(scales)
+
+        score = [[None] * HALVES for n in range(2)]
+        for n in range(2):
+            for h in range(HALVES):
+                score[n][h] = bank(2 * n + h, [P, I], "score%d%d" % (n, h))
+                cols = slice(h * P, (h + 1) * P)
+                nc.tensor.matmul_mx(
+                    score[n][h][:],
+                    lhsT=q_codes[n][:, cols].bitcast(FP8X4),
+                    lhsT_scale=q_scales[n][:, cols],
+                    rhs=kg_words[:].bitcast(FP4X4),
+                    rhs_scale=kg_bytes[:],
+                    start=True,
+                    stop=True,
+                )
+        a, ta = score
+
+        def turn(out, in_, start=True, stop=True):
+            nc.tensor.matmul(out, in_, ident[:], start=start, stop=stop, is_transpose=True)
+
+        a_sum = held.tile([P, HALVES, G], F32, name="a_sum")
+        sig = [held.tile([P, PACK, P], F32, name="sig%d" % h) for h in range(HALVES)]
+        for h in range(HALVES):
+            nc.scalar.activation(sig[h][:], a[h][:].rearrange("p (s r) -> p r s", r=PACK), ACT.Sigmoid)
+            nc.vector.tensor_reduce(a_sum[:, h, :], a[h][:].rearrange("p (g j) -> p g j", j=SPAN), AX.X, ALU.add)
+        neg_max = held.tile([P, HALVES], F32, name="neg_max")
+        nc.vector.tensor_reduce(neg_max[:], a_sum[:], AX.X, ALU.max, negate=True)
+        by_member = held.tile([P, SPAN, HALVES, G], F32, name="by_member")
+        for h in range(HALVES):
+            nc.scalar.copy(by_member[:, :, h, :], ta[h][:].rearrange("p (g j) -> p j g", j=SPAN))
+        warm_exp = held.tile([P, 1], F32, name="warm_exp")
+        nc.scalar.activation(warm_exp[:], by_member[:, 0, 1, 0:1], ACT.Exp, scale=0.0)
+        exp_bias = held.tile([P, HALVES], F32, name="exp_bias", tag="v_grouped0", align_bytes=64)
+        nc.scalar.activation(exp_bias[:], neg_max[:], ACT.Copy, scale=1.0 / SPAN)
+        p_span = held.tile([P, HALVES, G], F32, name="p_span")
+        p_sum = held.tile([P, HALVES], F32, name="p_sum")
+        for h in range(HALVES):
+            nc.scalar.activation(
+                p_span[:, h, :], a_sum[:, h, :], ACT.Exp, bias=exp_bias[:, h : h + 1], scale=1.0 / SPAN,
+                accum_out=p_sum[:, h : h + 1],
+            )
+        sums_bank = bank(6, [P, 2, P], "sums_bank")
+        for j in range(SPAN):
+            turn(sums_bank[:, 0, :], by_member[:, j, :, :].rearrange("p h g -> p (h g)"),
+                 start=(j == 0), stop=(j == SPAN - 1))
+        means_t = held.tile([P, P], F32, name="means_t")
+        nc.scalar.activation(means_t[:], sums_bank[:, 0, :], ACT.Copy, scale=1.0 / SPAN)
+        turn(sums_bank[:, 1, :], means_t[:])
+        ta_mean = sums_bank[:, 1, :].rearrange("p (h g) -> p h g", h=HALVES)
+
+        slope = [held.tile([P, PACK, P], F32, name="slope%d" % h) for h in range(HALVES)]
+        for h in range(HALVES):
+            nc.vector.scalar_tensor_tensor(
+                slope[h][:], sig[h][:], -1.0, ta[h][:].rearrange("p (s r) -> p r s", r=PACK), ALU.add, ALU.mult
+            )
+
+        sig_t = [bank(4 + j, [P, 2, Q], "sig_t%d" % j) for j in range(2)]
+        for h in range(HALVES):
+            for r in range(PACK):
+                turn(sig_t[r // 2][:, r % 2, h * P : (h + 1) * P], sig[h][:, r, :])
+        inner = [bank(h, [P, PACK, P], "inner%d" % h) for h in range(HALVES)]
+        for h in range(HALVES):
+            for r in range(PACK):
+                turn(inner[h][:, r, :], slope[h][:, r, :], start=(r == 0), stop=False)
+
+
+        inv_sum = held.tile([P, HALVES], F32, name="inv_sum", tag="plane1", align_bytes=64)
+        nc.vector.reciprocal(inv_sum[:], p_sum[:])
+        share_t_bank = bank(2, [P, Q], "share_t_bank")
+        share, centre, shift = [], [], []
+        for h in range(HALVES):
+            share.append(held.tile([P, G, 2], F32, name="share%d" % h))
+            nc.scalar.activation(
+                share[h][:], p_span[:, h, :].unsqueeze(2).to_broadcast([P, G, 2]), ACT.Copy, scale=inv_sum[:, h : h + 1]
+            )
+            turn(share_t_bank[:, h * P : (h + 1) * P], share[h][:].rearrange("p g d -> p (g d)"))
+        for h in range(HALVES):
+            centre.append(held.tile([P, 1], F32, name="centre%d" % h))
+            terms = held.tile([P, G], F32, name="terms%d" % h, tag="picked%d" % (PACK - 1 - h))
+            nc.vector.scalar_tensor_tensor(
+                terms[:], p_span[:, h, :], inv_sum[:, h : h + 1], ta_mean[:, h, :], ALU.mult, ALU.mult,
+                accum_out=centre[h][:],
+            )
+        share_t = held.tile([P, Q], F32, name="share_t")
+        nc.scalar.activation(share_t[:], share_t_bank[:], ACT.Copy, scale=-1.0)
+        for h in range(HALVES):
+            shift.append(held.tile([P, G, 2], F32, name="shift%d" % h))
+            nc.scalar.activation(
+                shift[h][:], ta_mean[:, h, :].unsqueeze(2).to_broadcast([P, G, 2]), ACT.Identity,
+                bias=centre[h][:], scale=-1.0,
+            )
+            for r in range(PACK):
+                turn(inner[h][:, r, :], shift[h][:].rearrange("p g d -> p (g d)"), start=False, stop=(r == PACK - 1))
+
+        v_grouped = [
+            held.tile([P, 2, P * PACK], BF16, name="v_grouped%d" % m, tag="v_grouped%d" % m, align_bytes=64)
+            for m in range(2)
+        ]
+        for t in range(PACK):
+            picked = held.tile([P, I], BF16, name="picked%d" % t, tag="picked%d" % t)
+            nc.vector.tensor_copy(picked[:], v_raw[t][:].indirect(offsets[:]))
+            pairs = picked[:].bitcast(F32)
+            turned = bank(7, [P, 2, P], "turned%d" % t)
+            for u in range(2):
+                turn(turned[:, u, :], pairs[:, u : I // 2 : 2])
+            nc.scalar.copy(
+                v_grouped[t // 2][:, t % 2, :].bitcast(F32).rearrange("p (e u) -> p e u", u=2),
+                turned[:].rearrange("p u e -> p e u"),
+            )
+
+        v_codes, v_scales = [], []
+
+        def quantise_values(m, tag):
+            v_codes.append(held.tile([P, 2, P], U32, name="v_codes%d" % m, tag=tag, align_bytes=64))
+            v_scales.append(held.tile([P, 2, P], U8, name="v_scales%d" % m, align_bytes=64))
+            nc.vector.quantize_mx(
+                v_codes[m][:].rearrange("p t e -> p (t e)").bitcast(FP8X4),
+                v_scales[m][:].rearrange("p t e -> p (t e)"),
+                v_grouped[m][:].rearrange("p t x -> p (t x)"),
+            )
+
+        quantise_values(0, "plane2")
+        outer = held.tile([P, PACK, Q], F32, name="outer", tag="plane%d" % (PACK - 1), align_bytes=64)
+        for r in range(PACK):
+            nc.vector.scalar_tensor_tensor(
+                outer[:, r, :], sig_t[r // 2][:, r % 2, :], os_col[:, r : r + 1], share_t[:], ALU.mult, ALU.mult
+            )
+
+        quantise_values(1, "v_codes1")
+        out_dealt = out_0.rearrange("(p t) q -> p t q", t=PACK)
+        out_words = out_1[0].rearrange("p c r -> p (c r)").bitcast(I32)
+        o_codes = held.tile([P, Q], U32, name="o_codes", align_bytes=64)
+        o_scales = held.tile([P, Q], U8, name="o_scales", align_bytes=64)
+        result_bank = []
+        for h in range(HALVES):
+            cols = slice(h * P, (h + 1) * P)
+            w_grouped = held.tile([P, P, PACK], BF16, name="w_grouped%d" % h, align_bytes=64)
+            nc.vector.tensor_tensor(
+                w_grouped[:].rearrange("p (c i) r -> p c r i", i=2),
+                outer[:, :, cols].rearrange("p r (c i) -> p c r i", i=2),
+                inner[h][:].rearrange("p r (c i) -> p c r i", i=2),
+                ALU.mult,
+            )
+            w_codes = held.tile([P, P], U32, name="w_codes%d" % h, align_bytes=64)
+            w_scales = held.tile([P, P], U8, name="w_scales%d" % h, align_bytes=64)
+            nc.vector.quantize_mx(w_codes[:].bitcast(FP8X4), w_scales[:], w_grouped[:].rearrange("p q r -> p (q r)"))
+            result_bank.append(bank(2 + h, [P, PACK, P], "result_bank%d" % h))
+            for t in range(PACK):
+                nc.tensor.matmul_mx(
+                    result_bank[h][:, t, :],
+                    lhsT=v_codes[t // 2][:, t % 2, :].bitcast(FP8X4),
+                    lhsT_scale=v_scales[t // 2][:, t % 2, :],
+                    rhs=w_codes[:].bitcast(FP8X4),
+                    rhs_scale=w_scales[:],
+                    start=True,
+                    stop=True,
+                )
+        for h in range(HALVES):
+            cols = slice(h * P, (h + 1) * P)
+            result = held.tile([P, PACK, P], F32, name="result%d" % h)
+            nc.scalar.copy(result[:], result_bank[h][:])
+            nc.sync.dma_start(out_dealt[:, :, cols], result[:])
+            o_grouped = held.tile([P, P, PACK], BF16, name="o_grouped%d" % h, align_bytes=64)
+            nc.vector.tensor_copy(
+                o_grouped[:].rearrange("p (c i) t -> p c t i", i=4), result[:].rearrange("p t (c i) -> p c t i", i=4)
+            )
+            nc.vector.quantize_mx(
+                o_codes[:, cols].bitcast(FP8X4), o_scales[:, cols], o_grouped[:].rearrange("p q t -> p (q t)")
+            )
+        nc.sync.dma_start(out_words, o_codes[:].bitcast(I32))
+        for quad in range(4):
+            queue = nc.scalar if quad % 2 == 0 else nc.sync
+            queue.dma_start(
+                out_2[0, 4 * quad : 4 * quad + 4, :].bitcast(I32),
+                o_scales[32 * quad : 32 * quad + 4, :].bitcast(I32),
+            )

@@ -28,10 +28,14 @@ def tile_attend_ttspanread_pl_kernel(tc, query, dquery, keys_words, keys_scales,
     nc = tc.nc
     with ExitStack() as ctx:
         held = ctx.enter_context(tc.tile_pool(name="held", bufs=1))
+        planes = ctx.enter_context(tc.tile_pool(name="planes", bufs=1))
         psum = ctx.enter_context(tc.psum_pool(name="psum", bufs=1))
 
         def bank(b, shape, name):
             return psum.tile(shape, F32, name=name, tag="bank%d" % b)
+
+        def on_plane(t, at, shape, dtype, name):
+            return planes.tile(shape, dtype, name=name, offset=t * T * 4 + at, align_bytes=64)
 
         offsets = held.tile([P, I // 16], U16, name="offsets")
         nc.sync.dma_start(offsets[:], offs)
@@ -49,20 +53,14 @@ def tile_attend_ttspanread_pl_kernel(tc, query, dquery, keys_words, keys_scales,
             )
         nc.sync.dma_start(q_raw[1][:], dquery.rearrange("(p j) q -> p j q", j=PACK))
         vals_dealt = vals.rearrange("(p t) n -> t p n", t=PACK)
-        v_raw = [held.tile([P, T], F32, name="v_raw%d" % t, tag="plane%d" % t, align_bytes=64) for t in range(PACK)]
-        nc.sync.dma_start(v_raw[0][:], vals_dealt[0])
+        v_raw = [on_plane(t, 0, [P, T], F32, "v_raw%d" % t) for t in range(PACK)]
         os_col = held.tile([P, PACK], F32, name="os_col")
         nc.sync.dma_start(os_col[:], slot_factor.rearrange("o (p t) -> (o p) t", t=PACK))
-        for t in range(1, PACK):
+        for t in range(PACK):
             nc.sync.dma_start(v_raw[t][:], vals_dealt[t])
 
         ident = held.tile([P, P], F32, name="ident")
         make_identity(nc, ident[:])
-
-        warm_in = held.tile([P, 1], F32, name="warm_in")
-        nc.vector.memset(warm_in[:], 0.0)
-        warm_out = held.tile([P, 1], F32, name="warm_out")
-        nc.scalar.activation(warm_out[:], warm_in[:], ACT.Sigmoid)
 
         kg_words = held.tile([P, I], U16, name="kg_words", align_bytes=64)
         nc.vector.tensor_copy(kg_words[:], key_words[:].indirect(offsets[:]))
@@ -72,7 +70,7 @@ def tile_attend_ttspanread_pl_kernel(tc, query, dquery, keys_words, keys_scales,
         q_codes, q_scales = [], []
         for n in range(2):
             grouped = held.tile([P, Q, PACK], BF16, name="q_grouped%d" % n, align_bytes=64)
-            nc.scalar.copy(
+            (nc.scalar.copy if n == 0 else nc.vector.tensor_copy)(
                 grouped[:].rearrange("p (c i) j -> p c j i", i=4),
                 q_raw[n][:].rearrange("p j (c i) -> p c j i", i=4),
             )
@@ -81,6 +79,9 @@ def tile_attend_ttspanread_pl_kernel(tc, query, dquery, keys_words, keys_scales,
             nc.vector.quantize_mx(codes[:].bitcast(FP8X4), scales[:], grouped[:].rearrange("p q j -> p (q j)"))
             q_codes.append(codes)
             q_scales.append(scales)
+
+        neg_os = held.tile([P, PACK], F32, name="neg_os")
+        nc.vector.tensor_scalar(neg_os[:], os_col[:], -1.0, None, ALU.mult)
 
         score = [[None] * HALVES for n in range(2)]
         for n in range(2):
@@ -101,41 +102,56 @@ def tile_attend_ttspanread_pl_kernel(tc, query, dquery, keys_words, keys_scales,
         def turn(out, in_, start=True, stop=True):
             nc.tensor.matmul(out, in_, ident[:], start=start, stop=stop, is_transpose=True)
 
-        a_sum = held.tile([P, HALVES, G], F32, name="a_sum")
+        def lay_by_member(n):
+            laid = held.tile([P, SPAN, HALVES, G], F32, name="by_member%d" % n)
+            for h in range(HALVES):
+                nc.scalar.copy(laid[:, :, h, :], score[n][h][:].rearrange("p (g j) -> p j g", j=SPAN))
+            return laid
+
+        def sum_members(laid, sums_bank):
+            for j in range(SPAN):
+                turn(sums_bank[:, 0, :], laid[:, j, :, :].rearrange("p h g -> p (h g)"),
+                     start=(j == 0), stop=(j == SPAN - 1))
+
+        def turn_back(sums_bank, means_t):
+            nc.scalar.activation(means_t[:], sums_bank[:, 0, :], ACT.Copy, scale=1.0 / SPAN)
+            turn(sums_bank[:, 1, :], means_t[:])
+            return sums_bank[:, 1, :].rearrange("p (h g) -> p h g", h=HALVES)
+
         sig = [held.tile([P, PACK, P], F32, name="sig%d" % h) for h in range(HALVES)]
         for h in range(HALVES):
             nc.scalar.activation(sig[h][:], a[h][:].rearrange("p (s r) -> p r s", r=PACK), ACT.Sigmoid)
-            nc.vector.tensor_reduce(a_sum[:, h, :], a[h][:].rearrange("p (g j) -> p g j", j=SPAN), AX.X, ALU.add)
-        neg_max = held.tile([P, HALVES], F32, name="neg_max")
-        nc.vector.tensor_reduce(neg_max[:], a_sum[:], AX.X, ALU.max, negate=True)
-        by_member = held.tile([P, SPAN, HALVES, G], F32, name="by_member")
-        for h in range(HALVES):
-            nc.scalar.copy(by_member[:, :, h, :], ta[h][:].rearrange("p (g j) -> p j g", j=SPAN))
-        warm_exp = held.tile([P, 1], F32, name="warm_exp")
-        nc.scalar.activation(warm_exp[:], by_member[:, 0, 1, 0:1], ACT.Exp, scale=0.0)
-        exp_bias = held.tile([P, HALVES], F32, name="exp_bias", tag="v_grouped0", align_bytes=64)
-        nc.scalar.activation(exp_bias[:], neg_max[:], ACT.Copy, scale=1.0 / SPAN)
-        p_span = held.tile([P, HALVES, G], F32, name="p_span")
-        p_sum = held.tile([P, HALVES], F32, name="p_sum")
-        for h in range(HALVES):
-            nc.scalar.activation(
-                p_span[:, h, :], a_sum[:, h, :], ACT.Exp, bias=exp_bias[:, h : h + 1], scale=1.0 / SPAN,
-                accum_out=p_sum[:, h : h + 1],
-            )
-        sums_bank = bank(6, [P, 2, P], "sums_bank")
-        for j in range(SPAN):
-            turn(sums_bank[:, 0, :], by_member[:, j, :, :].rearrange("p h g -> p (h g)"),
-                 start=(j == 0), stop=(j == SPAN - 1))
-        means_t = held.tile([P, P], F32, name="means_t")
-        nc.scalar.activation(means_t[:], sums_bank[:, 0, :], ACT.Copy, scale=1.0 / SPAN)
-        turn(sums_bank[:, 1, :], means_t[:])
-        ta_mean = sums_bank[:, 1, :].rearrange("p (h g) -> p h g", h=HALVES)
+        a_laid = lay_by_member(0)
+        a_sums_bank = bank(6, [P, 2, P], "a_sums_bank")
+        sum_members(a_laid, a_sums_bank)
+        a_mean = turn_back(a_sums_bank, held.tile([P, P], F32, name="a_means_t", tag="picked2"))
 
-        slope = [held.tile([P, PACK, P], F32, name="slope%d" % h) for h in range(HALVES)]
+        picked = []
+
+        def gather_plane(t):
+            picked.append(held.tile([P, I], BF16, name="picked%d" % t, tag="picked%d" % t))
+            nc.vector.tensor_copy(picked[t][:], v_raw[t][:].indirect(offsets[:]))
+
+        gather_plane(0)
+        slope = [on_plane(0, h * I * 4, [P, PACK, P], F32, "slope%d" % h) for h in range(HALVES)]
         for h in range(HALVES):
             nc.vector.scalar_tensor_tensor(
                 slope[h][:], sig[h][:], -1.0, ta[h][:].rearrange("p (s r) -> p r s", r=PACK), ALU.add, ALU.mult
             )
+        ta_laid = lay_by_member(1)
+        ta_sums_bank = bank(3, [P, 2, P], "ta_sums_bank")
+        sum_members(ta_laid, ta_sums_bank)
+
+        gather_plane(1)
+        neg_max = on_plane(1, 0, [P, HALVES], F32, "neg_max")
+        nc.vector.tensor_reduce(neg_max[:], a_mean, AX.X, ALU.max, negate=True)
+        p_span = held.tile([P, HALVES, G], F32, name="p_span", tag="v_grouped", align_bytes=64)
+        p_sum = held.tile([P, HALVES], F32, name="p_sum", tag="picked3")
+        for h in range(HALVES):
+            nc.scalar.activation(
+                p_span[:, h, :], a_mean[:, h, :], ACT.Exp, bias=neg_max[:, h : h + 1], accum_out=p_sum[:, h : h + 1]
+            )
+        ta_mean = turn_back(ta_sums_bank, on_plane(1, 0, [P, P], F32, "ta_means_t"))
 
         sig_t = [bank(4 + j, [P, 2, Q], "sig_t%d" % j) for j in range(2)]
         for h in range(HALVES):
@@ -147,73 +163,55 @@ def tile_attend_ttspanread_pl_kernel(tc, query, dquery, keys_words, keys_scales,
                 turn(inner[h][:, r, :], slope[h][:, r, :], start=(r == 0), stop=False)
 
 
-        inv_sum = held.tile([P, HALVES], F32, name="inv_sum", tag="plane1", align_bytes=64)
+        gather_plane(2)
+        inv_sum = on_plane(2, 0, [P, HALVES], F32, "inv_sum")
         nc.vector.reciprocal(inv_sum[:], p_sum[:])
         share_t_bank = bank(2, [P, Q], "share_t_bank")
-        share, centre, shift = [], [], []
+        share = held.tile([P, HALVES, G, 2], F32, name="share")
         for h in range(HALVES):
-            share.append(held.tile([P, G, 2], F32, name="share%d" % h))
             nc.scalar.activation(
-                share[h][:], p_span[:, h, :].unsqueeze(2).to_broadcast([P, G, 2]), ACT.Copy, scale=inv_sum[:, h : h + 1]
+                share[:, h, :, :], p_span[:, h, :].unsqueeze(2).to_broadcast([P, G, 2]), ACT.Copy,
+                scale=inv_sum[:, h : h + 1],
             )
-            turn(share_t_bank[:, h * P : (h + 1) * P], share[h][:].rearrange("p g d -> p (g d)"))
+            turn(share_t_bank[:, h * P : (h + 1) * P], share[:, h, :, :].rearrange("p g d -> p (g d)"))
+        sig_os = on_plane(1, 0, [P, PACK, Q], F32, "sig_os")
+        for r in range(PACK):
+            nc.scalar.activation(sig_os[:, r, :], sig_t[r // 2][:, r % 2, :], ACT.Copy, scale=neg_os[:, r : r + 1])
+
+        gather_plane(3)
+        outer = on_plane(3, 0, [P, PACK, Q], F32, "outer")
+        terms = on_plane(3, PACK * Q * 4, [P, HALVES, G], F32, "terms")
+        nc.vector.tensor_tensor(terms[:], share[:, :, :, 0], ta_mean, ALU.mult)
+        centre = held.tile([P, HALVES], F32, name="centre")
+        nc.vector.tensor_reduce(centre[:], terms[:], AX.X, ALU.add)
         for h in range(HALVES):
-            centre.append(held.tile([P, 1], F32, name="centre%d" % h))
-            terms = held.tile([P, G], F32, name="terms%d" % h, tag="picked%d" % (PACK - 1 - h))
-            nc.vector.scalar_tensor_tensor(
-                terms[:], p_span[:, h, :], inv_sum[:, h : h + 1], ta_mean[:, h, :], ALU.mult, ALU.mult,
-                accum_out=centre[h][:],
-            )
-        share_t = held.tile([P, Q], F32, name="share_t")
-        nc.scalar.activation(share_t[:], share_t_bank[:], ACT.Copy, scale=-1.0)
-        for h in range(HALVES):
-            shift.append(held.tile([P, G, 2], F32, name="shift%d" % h))
+            shift = held.tile([P, G, 2], F32, name="shift%d" % h)
             nc.scalar.activation(
-                shift[h][:], ta_mean[:, h, :].unsqueeze(2).to_broadcast([P, G, 2]), ACT.Identity,
-                bias=centre[h][:], scale=-1.0,
+                shift[:], ta_mean[:, h, :].unsqueeze(2).to_broadcast([P, G, 2]), ACT.Identity,
+                bias=centre[:, h : h + 1], scale=-1.0,
             )
             for r in range(PACK):
-                turn(inner[h][:, r, :], shift[h][:].rearrange("p g d -> p (g d)"), start=False, stop=(r == PACK - 1))
+                turn(inner[h][:, r, :], shift[:].rearrange("p g d -> p (g d)"), start=False, stop=(r == PACK - 1))
 
-        v_grouped = [
-            held.tile([P, 2, P * PACK], BF16, name="v_grouped%d" % m, tag="v_grouped%d" % m, align_bytes=64)
-            for m in range(2)
-        ]
-        for t in range(PACK):
-            picked = held.tile([P, I], BF16, name="picked%d" % t, tag="picked%d" % t)
-            nc.vector.tensor_copy(picked[:], v_raw[t][:].indirect(offsets[:]))
-            pairs = picked[:].bitcast(F32)
-            turned = bank(7, [P, 2, P], "turned%d" % t)
-            for u in range(2):
-                turn(turned[:, u, :], pairs[:, u : I // 2 : 2])
-            nc.scalar.copy(
-                v_grouped[t // 2][:, t % 2, :].bitcast(F32).rearrange("p (e u) -> p e u", u=2),
-                turned[:].rearrange("p u e -> p e u"),
-            )
+        v_grouped = held.tile([P, PACK, P, 2], F32, name="v_grouped", tag="v_grouped", align_bytes=64)
+        for m in range(2):
+            turned = bank(7 - m, [P, 2, 2, P], "turned%d" % m)
+            for t in range(2):
+                pairs = picked[2 * m + t][:].bitcast(F32)
+                for u in range(2):
+                    turn(turned[:, t, u, :], pairs[:, u : I // 2 : 2])
+            nc.scalar.copy(v_grouped[:, 2 * m : 2 * m + 2, :, :], turned[:].rearrange("p t u e -> p t e u"))
 
-        v_codes, v_scales = [], []
+        nc.vector.tensor_tensor(
+            outer[:], sig_os[:], share_t_bank[:].unsqueeze(1).to_broadcast([P, PACK, Q]), ALU.mult
+        )
 
-        def quantise_values(m, tag):
-            v_codes.append(held.tile([P, 2, P], U32, name="v_codes%d" % m, tag=tag, align_bytes=64))
-            v_scales.append(held.tile([P, 2, P], U8, name="v_scales%d" % m, align_bytes=64))
-            nc.vector.quantize_mx(
-                v_codes[m][:].rearrange("p t e -> p (t e)").bitcast(FP8X4),
-                v_scales[m][:].rearrange("p t e -> p (t e)"),
-                v_grouped[m][:].rearrange("p t x -> p (t x)"),
-            )
-
-        quantise_values(0, "plane2")
-        outer = held.tile([P, PACK, Q], F32, name="outer", tag="plane%d" % (PACK - 1), align_bytes=64)
-        for r in range(PACK):
-            nc.vector.scalar_tensor_tensor(
-                outer[:, r, :], sig_t[r // 2][:, r % 2, :], os_col[:, r : r + 1], share_t[:], ALU.mult, ALU.mult
-            )
-
-        quantise_values(1, "v_codes1")
         out_dealt = out_0.rearrange("(p t) q -> p t q", t=PACK)
         out_words = out_1[0].rearrange("p c r -> p (c r)").bitcast(I32)
         o_codes = held.tile([P, Q], U32, name="o_codes", align_bytes=64)
         o_scales = held.tile([P, Q], U8, name="o_scales", align_bytes=64)
+        v_codes = held.tile([P, PACK, P], U32, name="v_codes", align_bytes=64)
+        v_scales = held.tile([P, PACK, P], U8, name="v_scales", align_bytes=64)
         result_bank = []
         for h in range(HALVES):
             cols = slice(h * P, (h + 1) * P)
@@ -224,6 +222,12 @@ def tile_attend_ttspanread_pl_kernel(tc, query, dquery, keys_words, keys_scales,
                 inner[h][:].rearrange("p r (c i) -> p c r i", i=2),
                 ALU.mult,
             )
+            if h == 0:
+                nc.vector.quantize_mx(
+                    v_codes[:].rearrange("p t e -> p (t e)").bitcast(FP8X4),
+                    v_scales[:].rearrange("p t e -> p (t e)"),
+                    v_grouped[:].rearrange("p t e u -> p (t e u)").bitcast(BF16),
+                )
             w_codes = held.tile([P, P], U32, name="w_codes%d" % h, align_bytes=64)
             w_scales = held.tile([P, P], U8, name="w_scales%d" % h, align_bytes=64)
             nc.vector.quantize_mx(w_codes[:].bitcast(FP8X4), w_scales[:], w_grouped[:].rearrange("p q r -> p (q r)"))
@@ -231,8 +235,8 @@ def tile_attend_ttspanread_pl_kernel(tc, query, dquery, keys_words, keys_scales,
             for t in range(PACK):
                 nc.tensor.matmul_mx(
                     result_bank[h][:, t, :],
-                    lhsT=v_codes[t // 2][:, t % 2, :].bitcast(FP8X4),
-                    lhsT_scale=v_scales[t // 2][:, t % 2, :],
+                    lhsT=v_codes[:, t, :].bitcast(FP8X4),
+                    lhsT_scale=v_scales[:, t, :],
                     rhs=w_codes[:].bitcast(FP8X4),
                     rhs_scale=w_scales[:],
                     start=True,
@@ -241,18 +245,22 @@ def tile_attend_ttspanread_pl_kernel(tc, query, dquery, keys_words, keys_scales,
         for h in range(HALVES):
             cols = slice(h * P, (h + 1) * P)
             result = held.tile([P, PACK, P], F32, name="result%d" % h)
-            nc.scalar.copy(result[:], result_bank[h][:])
-            nc.sync.dma_start(out_dealt[:, :, cols], result[:])
             o_grouped = held.tile([P, P, PACK], BF16, name="o_grouped%d" % h, align_bytes=64)
-            nc.vector.tensor_copy(
-                o_grouped[:].rearrange("p (c i) t -> p c t i", i=4), result[:].rearrange("p t (c i) -> p c t i", i=4)
-            )
+            if h == 0:
+                nc.scalar.copy(result[:], result_bank[h][:])
+                nc.vector.tensor_copy(
+                    o_grouped[:].rearrange("p (c i) t -> p c t i", i=4), result[:].rearrange("p t (c i) -> p c t i", i=4)
+                )
+            else:
+                nc.scalar.copy(o_grouped[:], result_bank[h][:].rearrange("p t q -> p q t"))
+                nc.scalar.copy(result[:], result_bank[h][:])
+            (nc.sync if h == 0 else nc.scalar).dma_start(out_dealt[:, :, cols], result[:])
             nc.vector.quantize_mx(
                 o_codes[:, cols].bitcast(FP8X4), o_scales[:, cols], o_grouped[:].rearrange("p q t -> p (q t)")
             )
         nc.sync.dma_start(out_words, o_codes[:].bitcast(I32))
         for quad in range(4):
-            queue = nc.scalar if quad % 2 == 0 else nc.sync
+            queue = nc.scalar if quad == 3 else nc.sync
             queue.dma_start(
                 out_2[0, 4 * quad : 4 * quad + 4, :].bitcast(I32),
                 o_scales[32 * quad : 32 * quad + 4, :].bitcast(I32),

@@ -81,7 +81,7 @@ def tile_attend_ttspanread_pl_kernel(tc, query, dquery, keys_words, keys_scales,
             q_scales.append(scales)
 
         neg_os = held.tile([P, PACK], F32, name="neg_os")
-        nc.vector.tensor_scalar(neg_os[:], os_col[:], -1.0, None, ALU.mult)
+        nc.gpsimd.tensor_scalar(neg_os[:], os_col[:], -1.0, 0.0, ALU.mult, ALU.add)
 
         score = [[None] * HALVES for n in range(2)]
         for n in range(2):
@@ -102,56 +102,47 @@ def tile_attend_ttspanread_pl_kernel(tc, query, dquery, keys_words, keys_scales,
         def turn(out, in_, start=True, stop=True):
             nc.tensor.matmul(out, in_, ident[:], start=start, stop=stop, is_transpose=True)
 
-        def lay_by_member(n):
-            laid = held.tile([P, SPAN, HALVES, G], F32, name="by_member%d" % n)
-            for h in range(HALVES):
-                nc.scalar.copy(laid[:, :, h, :], score[n][h][:].rearrange("p (g j) -> p j g", j=SPAN))
-            return laid
-
-        def sum_members(laid, sums_bank):
-            for j in range(SPAN):
-                turn(sums_bank[:, 0, :], laid[:, j, :, :].rearrange("p h g -> p (h g)"),
-                     start=(j == 0), stop=(j == SPAN - 1))
-
-        def turn_back(sums_bank, means_t):
-            nc.scalar.activation(means_t[:], sums_bank[:, 0, :], ACT.Copy, scale=1.0 / SPAN)
-            turn(sums_bank[:, 1, :], means_t[:])
-            return sums_bank[:, 1, :].rearrange("p (h g) -> p h g", h=HALVES)
-
+        a_sum = held.tile([P, HALVES, G], F32, name="a_sum")
         sig = [held.tile([P, PACK, P], F32, name="sig%d" % h) for h in range(HALVES)]
         for h in range(HALVES):
+            nc.vector.tensor_reduce(a_sum[:, h, :], a[h][:].rearrange("p (g j) -> p g j", j=SPAN), AX.X, ALU.add)
             nc.scalar.activation(sig[h][:], a[h][:].rearrange("p (s r) -> p r s", r=PACK), ACT.Sigmoid)
-        a_laid = lay_by_member(0)
-        a_sums_bank = bank(6, [P, 2, P], "a_sums_bank")
-        sum_members(a_laid, a_sums_bank)
-        a_mean = turn_back(a_sums_bank, held.tile([P, P], F32, name="a_means_t", tag="picked2"))
+        neg_max = held.tile([P, HALVES], F32, name="neg_max")
+        nc.vector.tensor_reduce(neg_max[:], a_sum[:], AX.X, ALU.max, negate=True)
+        by_member = held.tile([P, SPAN, HALVES, G], F32, name="by_member")
+        for h in range(HALVES):
+            nc.scalar.copy(by_member[:, :, h, :], ta[h][:].rearrange("p (g j) -> p j g", j=SPAN))
+        exp_bias = held.tile([P, HALVES], F32, name="exp_bias", tag="after_exp")
+        nc.scalar.activation(exp_bias[:], neg_max[:], ACT.Copy, scale=1.0 / SPAN)
+        p_span = held.tile([P, HALVES, G], F32, name="p_span", tag="v_grouped", align_bytes=64)
+        p_sum = held.tile([P, HALVES], F32, name="p_sum", tag="picked3")
+        for h in range(HALVES):
+            nc.scalar.activation(
+                p_span[:, h, :], a_sum[:, h, :], ACT.Exp, bias=exp_bias[:, h : h + 1], scale=1.0 / SPAN,
+                accum_out=p_sum[:, h : h + 1],
+            )
+        sums_bank = bank(6, [P, 2, P], "sums_bank")
+        for j in range(SPAN):
+            turn(sums_bank[:, 0, :], by_member[:, j, :, :].rearrange("p h g -> p (h g)"),
+                 start=(j == 0), stop=(j == SPAN - 1))
+        means_t = held.tile([P, P], F32, name="means_t", tag="after_exp")
+        nc.scalar.activation(means_t[:], sums_bank[:, 0, :], ACT.Copy, scale=1.0 / SPAN)
+        turn(sums_bank[:, 1, :], means_t[:])
+        ta_mean = sums_bank[:, 1, :].rearrange("p (h g) -> p h g", h=HALVES)
 
         picked = []
 
-        def gather_plane(t):
-            picked.append(held.tile([P, I], BF16, name="picked%d" % t, tag="picked%d" % t))
-            nc.vector.tensor_copy(picked[t][:], v_raw[t][:].indirect(offsets[:]))
+        def gather_plane(t, into):
+            picked.append(into)
+            nc.vector.tensor_copy(into[:], v_raw[t][:].indirect(offsets[:]))
 
-        gather_plane(0)
+        gather_plane(0, held.tile([P, I], BF16, name="picked0"))
         slope = [on_plane(0, h * I * 4, [P, PACK, P], F32, "slope%d" % h) for h in range(HALVES)]
         for h in range(HALVES):
             nc.vector.scalar_tensor_tensor(
                 slope[h][:], sig[h][:], -1.0, ta[h][:].rearrange("p (s r) -> p r s", r=PACK), ALU.add, ALU.mult
             )
-        ta_laid = lay_by_member(1)
-        ta_sums_bank = bank(3, [P, 2, P], "ta_sums_bank")
-        sum_members(ta_laid, ta_sums_bank)
-
-        gather_plane(1)
-        neg_max = on_plane(1, 0, [P, HALVES], F32, "neg_max")
-        nc.vector.tensor_reduce(neg_max[:], a_mean, AX.X, ALU.max, negate=True)
-        p_span = held.tile([P, HALVES, G], F32, name="p_span", tag="v_grouped", align_bytes=64)
-        p_sum = held.tile([P, HALVES], F32, name="p_sum", tag="picked3")
-        for h in range(HALVES):
-            nc.scalar.activation(
-                p_span[:, h, :], a_mean[:, h, :], ACT.Exp, bias=neg_max[:, h : h + 1], accum_out=p_sum[:, h : h + 1]
-            )
-        ta_mean = turn_back(ta_sums_bank, on_plane(1, 0, [P, P], F32, "ta_means_t"))
+        gather_plane(1, held.tile([P, I], BF16, name="picked1"))
 
         sig_t = [bank(4 + j, [P, 2, Q], "sig_t%d" % j) for j in range(2)]
         for h in range(HALVES):
@@ -163,7 +154,7 @@ def tile_attend_ttspanread_pl_kernel(tc, query, dquery, keys_words, keys_scales,
                 turn(inner[h][:, r, :], slope[h][:, r, :], start=(r == 0), stop=False)
 
 
-        gather_plane(2)
+        gather_plane(2, held.tile([P, I], BF16, name="picked2"))
         inv_sum = on_plane(2, 0, [P, HALVES], F32, "inv_sum")
         nc.vector.reciprocal(inv_sum[:], p_sum[:])
         share_t_bank = bank(2, [P, Q], "share_t_bank")
@@ -174,17 +165,17 @@ def tile_attend_ttspanread_pl_kernel(tc, query, dquery, keys_words, keys_scales,
                 scale=inv_sum[:, h : h + 1],
             )
             turn(share_t_bank[:, h * P : (h + 1) * P], share[:, h, :, :].rearrange("p g d -> p (g d)"))
-        sig_os = on_plane(1, 0, [P, PACK, Q], F32, "sig_os")
+        sig_os = held.tile([P, PACK, Q], F32, name="sig_os", tag="after_exp")
         for r in range(PACK):
             nc.scalar.activation(sig_os[:, r, :], sig_t[r // 2][:, r % 2, :], ACT.Copy, scale=neg_os[:, r : r + 1])
 
-        gather_plane(3)
-        outer = on_plane(3, 0, [P, PACK, Q], F32, "outer")
-        terms = on_plane(3, PACK * Q * 4, [P, HALVES, G], F32, "terms")
-        nc.vector.tensor_tensor(terms[:], share[:, :, :, 0], ta_mean, ALU.mult)
+        terms = held.tile([P, HALVES, G], F32, name="terms", tag="picked3")
+        nc.vector.tensor_tensor(terms[:], p_span[:], ta_mean, ALU.mult)
+        tp_sum = held.tile([P, HALVES], F32, name="tp_sum")
+        nc.vector.tensor_reduce(tp_sum[:], terms[:], AX.X, ALU.add)
         centre = held.tile([P, HALVES], F32, name="centre")
-        nc.vector.tensor_reduce(centre[:], terms[:], AX.X, ALU.add)
         for h in range(HALVES):
+            nc.scalar.activation(centre[:, h : h + 1], tp_sum[:, h : h + 1], ACT.Copy, scale=inv_sum[:, h : h + 1])
             shift = held.tile([P, G, 2], F32, name="shift%d" % h)
             nc.scalar.activation(
                 shift[:], ta_mean[:, h, :].unsqueeze(2).to_broadcast([P, G, 2]), ACT.Identity,
@@ -193,6 +184,8 @@ def tile_attend_ttspanread_pl_kernel(tc, query, dquery, keys_words, keys_scales,
             for r in range(PACK):
                 turn(inner[h][:, r, :], shift[:].rearrange("p g d -> p (g d)"), start=False, stop=(r == PACK - 1))
 
+        gather_plane(3, held.tile([P, I], BF16, name="picked3", tag="picked3"))
+        outer = on_plane(3, 0, [P, PACK, Q], F32, "outer")
         v_grouped = held.tile([P, PACK, P, 2], F32, name="v_grouped", tag="v_grouped", align_bytes=64)
         for m in range(2):
             turned = bank(7 - m, [P, 2, 2, P], "turned%d" % m)

@@ -70,7 +70,7 @@ def tile_attend_ttspanread_pl_kernel(tc, query, dquery, keys_words, keys_scales,
         q_codes, q_scales = [], []
         for n in range(2):
             grouped = held.tile([P, Q, PACK], BF16, name="q_grouped%d" % n, align_bytes=64)
-            (nc.scalar.copy if n == 0 else nc.vector.tensor_copy)(
+            nc.scalar.copy(
                 grouped[:].rearrange("p (c i) j -> p c j i", i=4),
                 q_raw[n][:].rearrange("p j (c i) -> p c j i", i=4),
             )
@@ -79,9 +79,6 @@ def tile_attend_ttspanread_pl_kernel(tc, query, dquery, keys_words, keys_scales,
             nc.vector.quantize_mx(codes[:].bitcast(FP8X4), scales[:], grouped[:].rearrange("p q j -> p (q j)"))
             q_codes.append(codes)
             q_scales.append(scales)
-
-        neg_os = held.tile([P, PACK], F32, name="neg_os")
-        nc.gpsimd.tensor_scalar(neg_os[:], os_col[:], -1.0, 0.0, ALU.mult, ALU.add)
 
         score = [[None] * HALVES for n in range(2)]
         for n in range(2):
@@ -114,7 +111,7 @@ def tile_attend_ttspanread_pl_kernel(tc, query, dquery, keys_words, keys_scales,
             nc.scalar.copy(by_member[:, :, h, :], ta[h][:].rearrange("p (g j) -> p j g", j=SPAN))
         exp_bias = held.tile([P, HALVES], F32, name="exp_bias", tag="after_exp")
         nc.scalar.activation(exp_bias[:], neg_max[:], ACT.Copy, scale=1.0 / SPAN)
-        p_span = held.tile([P, HALVES, G], F32, name="p_span", tag="v_grouped", align_bytes=64)
+        p_span = held.tile([P, HALVES, G], F32, name="p_span")
         p_sum = held.tile([P, HALVES], F32, name="p_sum", tag="picked3")
         for h in range(HALVES):
             nc.scalar.activation(
@@ -137,12 +134,12 @@ def tile_attend_ttspanread_pl_kernel(tc, query, dquery, keys_words, keys_scales,
             nc.vector.tensor_copy(into[:], v_raw[t][:].indirect(offsets[:]))
 
         gather_plane(0, held.tile([P, I], BF16, name="picked0"))
-        slope = [on_plane(0, h * I * 4, [P, PACK, P], F32, "slope%d" % h) for h in range(HALVES)]
+        gather_plane(1, held.tile([P, I], BF16, name="picked1"))
+        slope = [on_plane(1, h * I * 4, [P, PACK, P], F32, "slope%d" % h) for h in range(HALVES)]
         for h in range(HALVES):
             nc.vector.scalar_tensor_tensor(
                 slope[h][:], sig[h][:], -1.0, ta[h][:].rearrange("p (s r) -> p r s", r=PACK), ALU.add, ALU.mult
             )
-        gather_plane(1, held.tile([P, I], BF16, name="picked1"))
 
         sig_t = [bank(4 + j, [P, 2, Q], "sig_t%d" % j) for j in range(2)]
         for h in range(HALVES):
@@ -158,16 +155,15 @@ def tile_attend_ttspanread_pl_kernel(tc, query, dquery, keys_words, keys_scales,
         inv_sum = on_plane(2, 0, [P, HALVES], F32, "inv_sum")
         nc.vector.reciprocal(inv_sum[:], p_sum[:])
         share_t_bank = bank(2, [P, Q], "share_t_bank")
-        share = held.tile([P, HALVES, G, 2], F32, name="share")
+        share = held.tile([P, HALVES, G, 2], F32, name="share", tag="v_grouped", align_bytes=64)
         for h in range(HALVES):
             nc.scalar.activation(
                 share[:, h, :, :], p_span[:, h, :].unsqueeze(2).to_broadcast([P, G, 2]), ACT.Copy,
                 scale=inv_sum[:, h : h + 1],
             )
             turn(share_t_bank[:, h * P : (h + 1) * P], share[:, h, :, :].rearrange("p g d -> p (g d)"))
-        sig_os = held.tile([P, PACK, Q], F32, name="sig_os", tag="after_exp")
-        for r in range(PACK):
-            nc.scalar.activation(sig_os[:, r, :], sig_t[r // 2][:, r % 2, :], ACT.Copy, scale=neg_os[:, r : r + 1])
+        share_t = held.tile([P, Q], F32, name="share_t")
+        nc.scalar.activation(share_t[:], share_t_bank[:], ACT.Copy, scale=-1.0)
 
         terms = held.tile([P, HALVES, G], F32, name="terms", tag="picked3")
         nc.vector.tensor_tensor(terms[:], p_span[:], ta_mean, ALU.mult)
@@ -195,9 +191,10 @@ def tile_attend_ttspanread_pl_kernel(tc, query, dquery, keys_words, keys_scales,
                     turn(turned[:, t, u, :], pairs[:, u : I // 2 : 2])
             nc.scalar.copy(v_grouped[:, 2 * m : 2 * m + 2, :, :], turned[:].rearrange("p t u e -> p t e u"))
 
-        nc.vector.tensor_tensor(
-            outer[:], sig_os[:], share_t_bank[:].unsqueeze(1).to_broadcast([P, PACK, Q]), ALU.mult
-        )
+        for r in range(PACK):
+            nc.vector.scalar_tensor_tensor(
+                outer[:, r, :], sig_t[r // 2][:, r % 2, :], os_col[:, r : r + 1], share_t[:], ALU.mult, ALU.mult
+            )
 
         out_dealt = out_0.rearrange("(p t) q -> p t q", t=PACK)
         out_words = out_1[0].rearrange("p c r -> p (c r)").bitcast(I32)
@@ -239,21 +236,17 @@ def tile_attend_ttspanread_pl_kernel(tc, query, dquery, keys_words, keys_scales,
             cols = slice(h * P, (h + 1) * P)
             result = held.tile([P, PACK, P], F32, name="result%d" % h)
             o_grouped = held.tile([P, P, PACK], BF16, name="o_grouped%d" % h, align_bytes=64)
-            if h == 0:
-                nc.scalar.copy(result[:], result_bank[h][:])
-                nc.vector.tensor_copy(
-                    o_grouped[:].rearrange("p (c i) t -> p c t i", i=4), result[:].rearrange("p t (c i) -> p c t i", i=4)
-                )
-            else:
-                nc.scalar.copy(o_grouped[:], result_bank[h][:].rearrange("p t q -> p q t"))
-                nc.scalar.copy(result[:], result_bank[h][:])
-            (nc.sync if h == 0 else nc.scalar).dma_start(out_dealt[:, :, cols], result[:])
+            nc.scalar.copy(result[:], result_bank[h][:])
+            nc.sync.dma_start(out_dealt[:, :, cols], result[:])
+            nc.vector.tensor_copy(
+                o_grouped[:].rearrange("p (c i) t -> p c t i", i=4), result[:].rearrange("p t (c i) -> p c t i", i=4)
+            )
             nc.vector.quantize_mx(
                 o_codes[:, cols].bitcast(FP8X4), o_scales[:, cols], o_grouped[:].rearrange("p q t -> p (q t)")
             )
         nc.sync.dma_start(out_words, o_codes[:].bitcast(I32))
         for quad in range(4):
-            queue = nc.scalar if quad == 3 else nc.sync
+            queue = nc.scalar if quad % 2 == 0 else nc.sync
             queue.dma_start(
                 out_2[0, 4 * quad : 4 * quad + 4, :].bitcast(I32),
                 o_scales[32 * quad : 32 * quad + 4, :].bitcast(I32),

from contextlib import ExitStack

import concourse.mybir as mybir
from concourse.masks import make_identity

D, E, T, I, Q, G = 512, 512, 2048, 512, 256, 64
FLOPS = 2 * (2 * Q * D * I + E * I * Q)

F32 = mybir.dt.float32
BF16 = mybir.dt.bfloat16
I32 = mybir.dt.int32
U32 = mybir.dt.uint32
U16 = mybir.dt.uint16
U8 = mybir.dt.uint8
FP8X4 = mybir.dt.float8_e4m3fn_x4
FP4X4 = mybir.dt.float4_e2m1fn_x4
ALU = mybir.AluOpType
ACT = mybir.ActivationFunctionType
AX = mybir.AxisListType

P = 128
PACK = 4
SPAN = I // G
HALVES = Q // P


def tile_attend_ttspanread_pl_kernel(tc, query, dquery, keys_words, keys_scales, slot_factor, vals, offs, out_0, out_1, out_2):
    nc = tc.nc
    with ExitStack() as ctx:
        held = ctx.enter_context(tc.tile_pool(name="held", bufs=1))
        planes = ctx.enter_context(tc.tile_pool(name="planes", bufs=1))
        psum = ctx.enter_context(tc.psum_pool(name="psum", bufs=1))

        def bank(b, shape, name):
            return psum.tile(shape, F32, name=name, tag="bank%d" % b)

        def on_plane(t, at, shape, dtype, name):
            return planes.tile(shape, dtype, name=name, offset=t * T * 4 + at, align_bytes=64)

        offsets = held.tile([P, I // 16], U16, name="offsets")
        nc.sync.dma_start(offsets[:], offs)
        key_words = held.tile([P, T], U16, name="key_words")
        nc.sync.dma_start(key_words[:].bitcast(I32), keys_words[0].bitcast(I32))
        key_bytes = held.tile([P, T], U8, name="key_bytes", tag="bytes_then_codes0", align_bytes=64)
        nc.vector.memset(key_bytes[:, : T // 2].bitcast(I32), 0)
        nc.gpsimd.memset(key_bytes[:, T // 2 :].bitcast(I32), 0)
        q_raw = [held.tile([P, PACK, Q], F32, name="q_raw%d" % n) for n in range(2)]
        nc.sync.dma_start(q_raw[0][:], query.rearrange("(p j) q -> p j q", j=PACK))
        for quad in range(4):
            nc.sync.dma_start(
                key_bytes[32 * quad : 32 * quad + 4, :].bitcast(I32),
                keys_scales[0, 4 * quad : 4 * quad + 4, :].bitcast(I32),
            )
        nc.sync.dma_start(q_raw[1][:], dquery.rearrange("(p j) q -> p j q", j=PACK))
        vals_dealt = vals.rearrange("(p t) n -> t p n", t=PACK)
        v_raw = [on_plane(t, 0, [P, T], F32, "v_raw%d" % t) for t in range(PACK)]
        os_col = held.tile([P, PACK], F32, name="os_col")
        nc.sync.dma_start(os_col[:], slot_factor.rearrange("o (p t) -> (o p) t", t=PACK))
        for t in range(PACK):
            nc.sync.dma_start(v_raw[t][:], vals_dealt[t])

        ident = held.tile([P, P], F32, name="ident")
        make_identity(nc, ident[:])

        kg_words = held.tile([P, I], U16, name="kg_words", align_bytes=64)
        nc.vector.tensor_copy(kg_words[:], key_words[:].indirect(offsets[:]))
        kg_bytes = held.tile([P, I], U8, name="kg_bytes", align_bytes=64)
        nc.vector.tensor_copy(kg_bytes[:], key_bytes[:].indirect(offsets[:]))

        q_codes, q_scales = [], []
        for n in range(2):
            grouped = held.tile([P, Q, PACK], BF16, name="q_grouped%d" % n, align_bytes=64)
            nc.scalar.copy(
                grouped[:].rearrange("p (c i) j -> p c j i", i=4),
                q_raw[n][:].rearrange("p j (c i) -> p c j i", i=4),
            )
            codes = held.tile([P, Q], U32, name="q_codes%d" % n, tag="bytes_then_codes%d" % n, align_bytes=64)
            scales = held.tile([P, Q], U8, name="q_scales%d" % n, align_bytes=64)
            nc.vector.quantize_mx(codes[:].bitcast(FP8X4), scales[:], grouped[:].rearrange("p q j -> p (q j)"))
            q_codes.append(codes)
            q_scales.append(scales)

        score = [[None] * HALVES for n in range(2)]
        for n in range(2):
            for h in range(HALVES):
                score[n][h] = bank(2 * n + h, [P, I], "score%d%d" % (n, h))
                cols = slice(h * P, (h + 1) * P)
                nc.tensor.matmul_mx(
                    score[n][h][:],
                    lhsT=q_codes[n][:, cols].bitcast(FP8X4),
                    lhsT_scale=q_scales[n][:, cols],
                    rhs=kg_words[:].bitcast(FP4X4),
                    rhs_scale=kg_bytes[:],
                    start=True,
                    stop=True,
                )
        a, ta = score

        def turn(out, in_, start=True, stop=True):
            nc.tensor.matmul(out, in_, ident[:], start=start, stop=stop, is_transpose=True)

        a_sum = held.tile([P, HALVES, G], F32, name="a_sum")
        sig = [held.tile([P, PACK, P], F32, name="sig%d" % h) for h in range(HALVES)]
        for h in range(HALVES):
            nc.vector.tensor_reduce(a_sum[:, h, :], a[h][:].rearrange("p (g j) -> p g j", j=SPAN), AX.X, ALU.add)
            nc.scalar.activation(sig[h][:], a[h][:].rearrange("p (s r) -> p r s", r=PACK), ACT.Sigmoid)
        neg_max = held.tile([P, HALVES], F32, name="neg_max")
        nc.vector.tensor_reduce(neg_max[:], a_sum[:], AX.X, ALU.max, negate=True)
        by_member = held.tile([P, SPAN, HALVES, G], F32, name="by_member")
        for h in range(HALVES):
            nc.scalar.copy(by_member[:, :, h, :], ta[h][:].rearrange("p (g j) -> p j g", j=SPAN))
        exp_bias = held.tile([P, HALVES], F32, name="exp_bias", tag="after_exp")
        nc.scalar.activation(exp_bias[:], neg_max[:], ACT.Copy, scale=1.0 / SPAN)
        p_span = held.tile([P, HALVES, G], F32, name="p_span")
        p_sum = held.tile([P, HALVES], F32, name="p_sum", tag="picked3")
        for h in range(HALVES):
            nc.scalar.activation(
                p_span[:, h, :], a_sum[:, h, :], ACT.Exp, bias=exp_bias[:, h : h + 1], scale=1.0 / SPAN,
                accum_out=p_sum[:, h : h + 1],
            )
        sums_bank = bank(6, [P, 2, P], "sums_bank")
        for j in range(SPAN):
            turn(sums_bank[:, 0, :], by_member[:, j, :, :].rearrange("p h g -> p (h g)"),
                 start=(j == 0), stop=(j == SPAN - 1))
        means_t = held.tile([P, P], F32, name="means_t", tag="after_exp")
        nc.scalar.activation(means_t[:], sums_bank[:, 0, :], ACT.Copy, scale=1.0 / SPAN)
        turn(sums_bank[:, 1, :], means_t[:])
        ta_mean = sums_bank[:, 1, :].rearrange("p (h g) -> p h g", h=HALVES)

        picked = []

        def gather_plane(t, into):
            picked.append(into)
            nc.vector.tensor_copy(into[:], v_raw[t][:].indirect(offsets[:]))

        gather_plane(0, held.tile([P, I], BF16, name="picked0"))
        gather_plane(1, held.tile([P, I], BF16, name="picked1"))
        slope = [on_plane(1, h * I * 4, [P, PACK, P], F32, "slope%d" % h) for h in range(HALVES)]
        for h in range(HALVES):
            nc.vector.scalar_tensor_tensor(
                slope[h][:], sig[h][:], -1.0, ta[h][:].rearrange("p (s r) -> p r s", r=PACK), ALU.add, ALU.mult
            )

        sig_t = [bank(4 + j, [P, 2, Q], "sig_t%d" % j) for j in range(2)]
        for h in range(HALVES):
            for r in range(PACK):
                turn(sig_t[r // 2][:, r % 2, h * P : (h + 1) * P], sig[h][:, r, :])
        inner = [bank(h, [P, PACK, P], "inner%d" % h) for h in range(HALVES)]
        for h in range(HALVES):
            for r in range(PACK):
                turn(inner[h][:, r, :], slope[h][:, r, :], start=(r == 0), stop=False)


        gather_plane(2, held.tile([P, I], BF16, name="picked2"))
        inv_sum = on_plane(2, 0, [P, HALVES], F32, "inv_sum")
        nc.vector.reciprocal(inv_sum[:], p_sum[:])
        share_t_bank = bank(2, [P, Q], "share_t_bank")
        share = held.tile([P, HALVES, G, 2], F32, name="share", tag="v_grouped", align_bytes=64)
        for h in range(HALVES):
            nc.scalar.activation(
                share[:, h, :, :], p_span[:, h, :].unsqueeze(2).to_broadcast([P, G, 2]), ACT.Copy,
                scale=inv_sum[:, h : h + 1],
            )
            turn(share_t_bank[:, h * P : (h + 1) * P], share[:, h, :, :].rearrange("p g d -> p (g d)"))
        share_t = held.tile([P, Q], F32, name="share_t")
        nc.scalar.activation(share_t[:], share_t_bank[:], ACT.Copy, scale=-1.0)

        terms = held.tile([P, HALVES, G], F32, name="terms", tag="picked3")
        nc.vector.tensor_tensor(terms[:], p_span[:], ta_mean, ALU.mult)
        tp_sum = held.tile([P, HALVES], F32, name="tp_sum")
        nc.vector.tensor_reduce(tp_sum[:], terms[:], AX.X, ALU.add)
        centre = held.tile([P, HALVES], F32, name="centre")
        for h in range(HALVES):
            nc.scalar.activation(centre[:, h : h + 1], tp_sum[:, h : h + 1], ACT.Copy, scale=inv_sum[:, h : h + 1])
            shift = held.tile([P, G, 2], F32, name="shift%d" % h)
            nc.scalar.activation(
                shift[:], ta_mean[:, h, :].unsqueeze(2).to_broadcast([P, G, 2]), ACT.Identity,
                bias=centre[:, h : h + 1], scale=-1.0,
            )
            for r in range(PACK):
                turn(inner[h][:, r, :], shift[:].rearrange("p g d -> p (g d)"), start=False, stop=(r == PACK - 1))

        gather_plane(3, held.tile([P, I], BF16, name="picked3", tag="picked3"))
        outer = on_plane(3, 0, [P, PACK, Q], F32, "outer")
        v_grouped = held.tile([P, PACK, P, 2], F32, name="v_grouped", tag="v_grouped", align_bytes=64)
        for m in range(2):
            turned = bank(7 - m, [P, 2, 2, P], "turned%d" % m)
            for t in range(2):
                pairs = picked[2 * m + t][:].bitcast(F32)
                for u in range(2):
                    turn(turned[:, t, u, :], pairs[:, u : I // 2 : 2])
            nc.scalar.copy(v_grouped[:, 2 * m : 2 * m + 2, :, :], turned[:].rearrange("p t u e -> p t e u"))

        for r in range(PACK):
            nc.vector.scalar_tensor_tensor(
                outer[:, r, :], sig_t[r // 2][:, r % 2, :], os_col[:, r : r + 1], share_t[:], ALU.mult, ALU.mult
            )

        out_dealt = out_0.rearrange("(p t) q -> p t q", t=PACK)
        out_words = out_1[0].rearrange("p c r -> p (c r)").bitcast(I32)
        o_codes = held.tile([P, Q], U32, name="o_codes", align_bytes=64)
        o_scales = held.tile([P, Q], U8, name="o_scales", align_bytes=64)
        v_codes = held.tile([P, PACK, P], U32, name="v_codes", align_bytes=64)
        v_scales = held.tile([P, PACK, P], U8, name="v_scales", align_bytes=64)
        result_bank = []
        for h in range(HALVES):
            cols = slice(h * P, (h + 1) * P)
            w_grouped = held.tile([P, P, PACK], BF16, name="w_grouped%d" % h, align_bytes=64)
            nc.vector.tensor_tensor(
                w_grouped[:].rearrange("p (c i) r -> p c r i", i=2),
                outer[:, :, cols].rearrange("p r (c i) -> p c r i", i=2),
                inner[h][:].rearrange("p r (c i) -> p c r i", i=2),
                ALU.mult,
            )
            if h == 0:
                nc.vector.quantize_mx(
                    v_codes[:].rearrange("p t e -> p (t e)").bitcast(FP8X4),
                    v_scales[:].rearrange("p t e -> p (t e)"),
                    v_grouped[:].rearrange("p t e u -> p (t e u)").bitcast(BF16),
                )
            w_codes = held.tile([P, P], U32, name="w_codes%d" % h, align_bytes=64)
            w_scales = held.tile([P, P], U8, name="w_scales%d" % h, align_bytes=64)
            nc.vector.quantize_mx(w_codes[:].bitcast(FP8X4), w_scales[:], w_grouped[:].rearrange("p q r -> p (q r)"))
            result_bank.append(bank(2 + h, [P, PACK, P], "result_bank%d" % h))
            for t in range(PACK):
                nc.tensor.matmul_mx(
                    result_bank[h][:, t, :],
                    lhsT=v_codes[:, t, :].bitcast(FP8X4),
                    lhsT_scale=v_scales[:, t, :],
                    rhs=w_codes[:].bitcast(FP8X4),
                    rhs_scale=w_scales[:],
                    start=True,
                    stop=True,
                )
        for h in range(HALVES):
            cols = slice(h * P, (h + 1) * P)
            result = held.tile([P, PACK, P], F32, name="result%d" % h)
            o_grouped = held.tile([P, P, PACK], BF16, name="o_grouped%d" % h, align_bytes=64)
            nc.scalar.copy(result[:], result_bank[h][:])
            nc.sync.dma_start(out_dealt[:, :, cols], result[:])
            nc.vector.tensor_copy(
                o_grouped[:].rearrange("p (c i) t -> p c t i", i=4), result[:].rearrange("p t (c i) -> p c t i", i=4)
            )
            nc.vector.quantize_mx(
                o_codes[:, cols].bitcast(FP8X4), o_scales[:, cols], o_grouped[:].rearrange("p q t -> p (q t)")
            )
        nc.sync.dma_start(out_words, o_codes[:].bitcast(I32))
        for quad in range(4):
            queue = nc.scalar if quad % 2 == 0 else nc.sync
            queue.dma_start(
                out_2[0, 4 * quad : 4 * quad + 4, :].bitcast(I32),
                o_scales[32 * quad : 32 * quad + 4, :].bitcast(I32),
            )
